import numpy as np
import ml_dtypes


def mxq(x, axis, fmt="e4m3"):
    dtype, down = {"e4m3": (ml_dtypes.float8_e4m3fn, 7), "e5m2": (ml_dtypes.float8_e5m2, 14)}[fmt]
    v = np.moveaxis(np.asarray(x, np.float32).astype(ml_dtypes.bfloat16).astype(np.float64), axis, -1)
    blocks = v.reshape(v.shape[:-1] + (-1, 32))
    amax = np.abs(blocks).max(-1, keepdims=True)
    byte = np.maximum(np.where(amax > 0, np.frexp(amax)[1] - 1 + 127, 0) - down, 1)
    scale = np.exp2(byte - 127.0)
    codes = (blocks / scale).astype(np.float32).astype(dtype).astype(np.float64)
    return np.moveaxis((codes * scale).reshape(v.shape), -1, axis)


WIDE = False


def mx_kscale(k):
    if not WIDE:
        return np.ones(k)
    levels = np.array([10, -10, 5, -5, 0])
    if k % 512:
        return np.exp2(np.random.permutation(np.resize(levels, k // 32))).repeat(32)
    a = np.empty((k // 512, 16))
    for p in range(k // 512):
        a[p, :8] = np.random.permutation(np.resize(levels, 8))
        for g in range(8):
            far = levels[np.abs(levels - a[p, g]) >= 10]
            a[p, g + 8] = far[np.random.randint(len(far))]
    return np.exp2(a.ravel()).repeat(32)


def f64(x):
    return np.asarray(x).astype(np.float64)


def striped(idx):
    return np.tile(np.asarray(idx).reshape(-1, 16).T, (8, 1)).astype(np.uint16)


def unstriped(offs):
    return offs[:16].T.reshape(-1).astype(np.int64)


E2M1 = np.array([0.0, 0.5, 1.0, 1.5, 2.0, 3.0, 4.0, 6.0, -0.0, -0.5, -1.0, -1.5, -2.0, -3.0, -4.0, -6.0])


def pack_weight(w, fmt):
    k, n = w.shape
    w = f64(np.asarray(w, np.float32).astype(ml_dtypes.bfloat16)).reshape(k // 32, 32, n)
    amax = np.abs(w).max(1)
    if fmt == "e4m3":
        byte = np.frexp(amax)[1] - 1 + 127 - 7
    else:
        mant, ex = np.frexp(amax / 6.0)
        byte = np.where(mant > 0.5, ex, ex - 1) + 127
    byte = np.clip(np.where(amax > 0, byte, 1), 1, 254)
    scaled = (w * np.exp2(127.0 - byte)[:, None, :]).reshape(k, n).astype(np.float32)
    by_word = np.ascontiguousarray(scaled.reshape(k // 512, 128, 4, n).transpose(0, 1, 3, 2))
    if fmt == "e4m3":
        words = by_word.astype(ml_dtypes.float8_e4m3fn).view(np.uint8)
    else:
        c = by_word.astype(ml_dtypes.float4_e2m1fn).view(np.uint8) & 0xF
        words = (c[..., 0::2] | (c[..., 1::2] << 4)).reshape(k // 512, 128, 2 * n)
    return np.ascontiguousarray(words), np.ascontiguousarray(byte.astype(np.uint8).reshape(k // 512, 16, n))


def unpack_weight(words, scales, fmt):
    g, _, n = scales.shape
    words = np.ascontiguousarray(words).reshape(g, 128, n, -1)
    if fmt == "e4m3":
        vals = words.view(ml_dtypes.float8_e4m3fn).astype(np.float64)
    else:
        nib = np.empty((g, 128, n, 4), np.uint8)
        nib[..., 0::2] = words & 0xF
        nib[..., 1::2] = words >> 4
        vals = E2M1[nib]
    vals = vals * np.repeat(np.exp2(scales.astype(np.float64) - 127.0), 8, axis=1)[..., None]
    return vals.transpose(0, 1, 3, 2).reshape(g * 512, n)


K, T, V, J, N, E = 512, 1024, 512, 256, 256, 512


def setup_inputs():
    n = np.random.standard_normal
    idx = np.random.permutation(T)[:J]
    idx2 = np.random.permutation(V)[:J]
    idx3 = np.random.permutation(E)[:J]
    fk = mx_kscale(K)
    wp = pack_weight(n((K, N)) * 1 / np.sqrt(K) / fk[:, None], "e2m1")
    return {
        "ca": (np.random.randint(-7, 8, (K, T)).astype(np.float64)).astype(np.float32),
        "cb": (np.random.randint(-7, 8, (K, V)).astype(np.float64)).astype(np.float32),
        "sa": (np.random.uniform(0.1, 0.4, (K, 1)) * fk[:, None]).astype(np.float32),
        "sb": (np.random.uniform(0.1, 0.4, (K, 1)) * fk[:, None]).astype(np.float32),
        "w_words": wp[0],
        "w_scales": wp[1],
        "so": (np.random.uniform(0.5, 1.6, (N, 1))).astype(np.float32),
        "offs": striped(idx),
        "offs2": striped(idx2),
        "offs3": striped(idx3),
    }


def reference(ca, cb, sa, sb, w_words, w_scales, so, offs, offs2, offs3):
    idx = unstriped(offs)
    idx2 = unstriped(offs2)
    idx3 = unstriped(offs3)
    wu = unpack_weight(w_words, w_scales, "e2m1")
    x1 = f64(ca)[:, idx] * f64(sa)
    x2 = f64(cb)[:, idx2] * f64(sb)
    x1q = mxq(x1, 0, "e4m3")
    x2q = mxq(x2, 0, "e4m3")
    p = wu.T @ x1q + wu.T @ x2q
    y = np.zeros((N, E))
    y[:, idx3] = p * f64(so)
    return y

@@ -1,0 +1,124 @@
+from contextlib import ExitStack
+
+import concourse.mybir as mybir
+
+K, T, V, J, N, E = 512, 1024, 512, 256, 256, 512
+FLOPS = 2 * 2 * K * N * J
+
+F32 = mybir.dt.float32
+BF16 = mybir.dt.bfloat16
+I32 = mybir.dt.int32
+U32 = mybir.dt.uint32
+U16 = mybir.dt.uint16
+U8 = mybir.dt.uint8
+FP8X4 = mybir.dt.float8_e4m3fn_x4
+FP4X4 = mybir.dt.float4_e2m1fn_x4
+COPY = mybir.ActivationFunctionType.Copy
+
+P = 128
+PACK = 4
+HALF = 128
+LIST_COLS = HALF // 16
+
+
+def tile_list_twocodebooks_kernel(tc, ca, cb, sa, sb, w_words, w_scales, so, offs, offs2, offs3, out):
+    nc = tc.nc
+    halves = range(J // HALF)
+    row_tiles = range(N // P)
+
+    with ExitStack() as ctx:
+        keep = ctx.enter_context(tc.tile_pool(name="keep", bufs=1))
+        psum = ctx.enter_context(tc.psum_pool(name="psum", bufs=1))
+
+        list_a = keep.tile([P, J // 16], U16, name="list_a")
+        list_b = keep.tile([P, J // 16], U16, name="list_b")
+        list_out = keep.tile([P, J // 16], U16, name="list_out")
+        step_a = keep.tile([P, PACK], F32, name="step_a")
+        step_b = keep.tile([P, PACK], F32, name="step_b")
+        gain = keep.tile([P, N // P], F32, name="gain")
+        table_a = [keep.tile([P, T], F32, name=f"table_a{r}") for r in range(PACK)]
+        table_b = [keep.tile([P, V], F32, name=f"table_b{r}") for r in range(PACK)]
+        w_codes = keep.tile([P, 2 * N], U8, name="w_codes", align_bytes=64)
+        w_rows = keep.tile([4, 4, N // 4], I32, name="w_rows")
+        w_plane = keep.tile([P, N], U8, name="w_plane", align_bytes=64)
+        pages = [keep.tile([P, E], F32, name=f"page{m}") for m in row_tiles]
+
+        ca_rows = ca.rearrange("(p r) t -> r p t", r=PACK)
+        cb_rows = cb.rearrange("(p r) v -> r p v", r=PACK)
+
+        nc.scalar.dma_start(step_b[:], sb.rearrange("(p r) o -> p (r o)", r=PACK))
+        nc.sync.dma_start(table_b[0][:], cb_rows[0])
+        nc.sync.dma_start(list_b[:], offs2)
+        for r in range(1, PACK):
+            nc.sync.dma_start(table_b[r][:], cb_rows[r])
+        nc.sync.dma_start(list_a[:], offs)
+        for r in range(PACK):
+            nc.sync.dma_start(table_a[r][:], ca_rows[r])
+        nc.sync.dma_start(w_codes[:].bitcast(I32), w_words[0].bitcast(I32))
+        nc.sync.dma_start(list_out[:], offs3)
+        nc.gpsimd.dma_start(step_a[:], sa.rearrange("(p r) o -> p (r o)", r=PACK))
+        nc.gpsimd.dma_start(w_rows[:], w_scales[0].bitcast(I32).rearrange("(q r) c -> r q c", r=4))
+        with nc.allow_non_contiguous_dma(reason="one float a partition and row tile"):
+            nc.gpsimd.dma_start(gain[:], so.rearrange("(m p) o -> p (m o)", p=P))
+
+        nc.vector.memset(w_plane[:].bitcast(I32), 0)
+        for m in row_tiles:
+            nc.vector.memset(pages[m][:], 0.0)
+        for q in range(4):
+            nc.vector.tensor_copy(w_plane[32 * q : 32 * q + 4, :].bitcast(I32), w_rows[:, q, :])
+
+        x = {}
+        codes = {}
+        scales = {}
+        for name in ("a", "b"):
+            for h in halves:
+                x[name, h] = keep.tile([P, PACK * HALF], BF16, name=f"x_{name}{h}", align_bytes=64)
+                codes[name, h] = keep.tile([P, HALF], U32, name=f"codes_{name}{h}", align_bytes=64)
+                scales[name, h] = keep.tile([P, HALF], U8, name=f"scales_{name}{h}", align_bytes=64)
+        acc = {(m, h): psum.tile([P, HALF], F32, name=f"acc{m}{h}") for h in halves for m in row_tiles}
+        sums = {(m, h): keep.tile([P, HALF], F32, name=f"sums{m}{h}") for h in halves for m in row_tiles}
+
+        def part(lst, h):
+            return lst[:, h * LIST_COLS : (h + 1) * LIST_COLS]
+
+        def fetch(name, table, lst, step, r, h):
+            nc.scalar.activation(
+                x[name, h][:, r : PACK * HALF : PACK],
+                table[r][:].indirect(part(lst, h)),
+                COPY,
+                scale=step[:, r : r + 1],
+            )
+
+        def multiply(name, h, first):
+            nc.vector.quantize_mx(
+                out=codes[name, h][:].bitcast(FP8X4), scales=scales[name, h][:], in_=x[name, h][:]
+            )
+            for m in row_tiles:
+                nc.tensor.matmul_mx(
+                    out=acc[m, h][:],
+                    lhsT=w_codes[:, 2 * m * P : 2 * (m + 1) * P].bitcast(FP4X4),
+                    lhsT_scale=w_plane[:, m * P : (m + 1) * P],
+                    rhs=codes[name, h][:].bitcast(FP8X4),
+                    rhs_scale=scales[name, h][:],
+                    start=first,
+                    stop=not first,
+                )
+
+        for r in range(PACK):
+            for h in halves:
+                fetch("b", table_b, list_b, step_b, r, h)
+        for h in halves:
+            multiply("b", h, True)
+        for r, h in ((0, 0), (0, 1), (1, 0), (1, 1), (2, 0), (3, 0), (3, 1), (2, 1)):
+            fetch("a", table_a, list_a, step_a, r, h)
+        for h in halves:
+            multiply("a", h, False)
+            for m in row_tiles:
+                nc.vector.tensor_copy(sums[m, h][:], acc[m, h][:])
+        for h in halves:
+            for m in row_tiles:
+                nc.scalar.activation(
+                    pages[m][:].indirect(part(list_out, h)), sums[m, h][:], COPY, scale=gain[:, m : m + 1]
+                )
+        for m in row_tiles:
+            nc.sync.dma_start(out[m * P : (m + 1) * P, :], pages[m][:])

@@ -61,6 +61,10 @@ def tile_list_twocodebooks_kernel(tc, ca, cb, sa, sb, w_words, w_scales, so, off
         with nc.allow_non_contiguous_dma(reason="one float a partition and row tile"):
             nc.gpsimd.dma_start(gain[:], so.rearrange("(m p) o -> p (m o)", p=P))
 
+        warm_in = keep.tile([P, 1], F32, name="warm_in")
+        warm_out = keep.tile([P, 1], F32, name="warm_out")
+        nc.vector.memset(warm_in[:], 0.0)
+        nc.scalar.activation(warm_out[:], warm_in[:], COPY)
         nc.vector.memset(w_plane[:].bitcast(I32), 0)
         for m in row_tiles:
             nc.vector.memset(pages[m][:], 0.0)

@@ -51,15 +51,17 @@ def tile_list_twocodebooks_kernel(tc, ca, cb, sa, sb, w_words, w_scales, so, off
         nc.sync.dma_start(list_b[:], offs2)
         for r in range(1, PACK):
             nc.sync.dma_start(table_b[r][:], cb_rows[r])
+        nc.sync.dma_start(table_a[0][:], ca_rows[0])
         nc.sync.dma_start(list_a[:], offs)
-        for r in range(PACK):
+        nc.sync.dma_start(step_a[:], sa.rearrange("(p r) o -> p (r o)", r=PACK))
+        nc.sync.dma_start(table_a[1][:], ca_rows[1])
+        nc.sync.dma_start(w_rows[:], w_scales[0].bitcast(I32).rearrange("(q r) c -> r q c", r=4))
+        for r in range(2, PACK):
             nc.sync.dma_start(table_a[r][:], ca_rows[r])
         nc.sync.dma_start(w_codes[:].bitcast(I32), w_words[0].bitcast(I32))
         nc.sync.dma_start(list_out[:], offs3)
-        nc.gpsimd.dma_start(step_a[:], sa.rearrange("(p r) o -> p (r o)", r=PACK))
-        nc.gpsimd.dma_start(w_rows[:], w_scales[0].bitcast(I32).rearrange("(q r) c -> r q c", r=4))
         with nc.allow_non_contiguous_dma(reason="one float a partition and row tile"):
-            nc.gpsimd.dma_start(gain[:], so.rearrange("(m p) o -> p (m o)", p=P))
+            nc.sync.dma_start(gain[:], so.rearrange("(m p) o -> p (m o)", p=P))
 
         warm_in = keep.tile([P, 1], F32, name="warm_in")
         warm_out = keep.tile([P, 1], F32, name="warm_out")
@@ -71,58 +73,79 @@ def tile_list_twocodebooks_kernel(tc, ca, cb, sa, sb, w_words, w_scales, so, off
         for q in range(4):
             nc.vector.tensor_copy(w_plane[32 * q : 32 * q + 4, :].bitcast(I32), w_rows[:, q, :])
 
-        x = {}
-        codes = {}
-        scales = {}
-        for name in ("a", "b"):
-            for h in halves:
-                x[name, h] = keep.tile([P, PACK * HALF], BF16, name=f"x_{name}{h}", align_bytes=64)
-                codes[name, h] = keep.tile([P, HALF], U32, name=f"codes_{name}{h}", align_bytes=64)
-                scales[name, h] = keep.tile([P, HALF], U8, name=f"scales_{name}{h}", align_bytes=64)
-        acc = {(m, h): psum.tile([P, HALF], F32, name=f"acc{m}{h}") for h in halves for m in row_tiles}
-        sums = {(m, h): keep.tile([P, HALF], F32, name=f"sums{m}{h}") for h in halves for m in row_tiles}
+        x_a = keep.tile([P, PACK * J], BF16, name="x_a", align_bytes=64)
+        x_b = keep.tile([P, PACK * J], BF16, name="x_b", align_bytes=64)
 
-        def part(lst, h):
-            return lst[:, h * LIST_COLS : (h + 1) * LIST_COLS]
-
-        def fetch(name, table, lst, step, r, h):
+        def fetch(x, table, lst, scale, r, lo, hi):
             nc.scalar.activation(
-                x[name, h][:, r : PACK * HALF : PACK],
-                table[r][:].indirect(part(lst, h)),
+                x[:, PACK * lo + r : PACK * hi : PACK],
+                table[r][:].indirect(lst[:, lo // 16 : hi // 16]),
                 COPY,
-                scale=step[:, r : r + 1],
+                scale=scale,
             )
 
-        def multiply(name, h, first):
-            nc.vector.quantize_mx(
-                out=codes[name, h][:].bitcast(FP8X4), scales=scales[name, h][:], in_=x[name, h][:]
+        def quantise(codes, scales, x, lo, hi):
+            nc.vector.quantize_mx(out=codes.bitcast(FP8X4), scales=scales, in_=x[:, PACK * lo : PACK * hi])
+
+        def multiply(acc, m, codes, scales, first):
+            nc.tensor.matmul_mx(
+                out=acc[:],
+                lhsT=w_codes[:, 2 * m * P : 2 * (m + 1) * P].bitcast(FP4X4),
+                lhsT_scale=w_plane[:, m * P : (m + 1) * P],
+                rhs=codes.bitcast(FP8X4),
+                rhs_scale=scales,
+                start=first,
+                stop=not first,
             )
+
+        def put(h, accs):
             for m in row_tiles:
-                nc.tensor.matmul_mx(
-                    out=acc[m, h][:],
-                    lhsT=w_codes[:, 2 * m * P : 2 * (m + 1) * P].bitcast(FP4X4),
-                    lhsT_scale=w_plane[:, m * P : (m + 1) * P],
-                    rhs=codes[name, h][:].bitcast(FP8X4),
-                    rhs_scale=scales[name, h][:],
-                    start=first,
-                    stop=not first,
+                sums = keep.tile([P, HALF], F32, name=f"sums{m}{h}")
+                nc.vector.tensor_copy(sums[:], accs[m][:])
+                nc.scalar.activation(
+                    pages[m][:].indirect(list_out[:, h * LIST_COLS : (h + 1) * LIST_COLS]),
+                    sums[:],
+                    COPY,
+                    scale=gain[:, m : m + 1],
                 )
 
         for r in range(PACK):
-            for h in halves:
-                fetch("b", table_b, list_b, step_b, r, h)
-        for h in halves:
-            multiply("b", h, True)
-        for r, h in ((0, 0), (0, 1), (1, 0), (1, 1), (2, 0), (3, 0), (3, 1), (2, 1)):
-            fetch("a", table_a, list_a, step_a, r, h)
-        for h in halves:
-            multiply("a", h, False)
-            for m in row_tiles:
-                nc.vector.tensor_copy(sums[m, h][:], acc[m, h][:])
-        for h in halves:
-            for m in row_tiles:
-                nc.scalar.activation(
-                    pages[m][:].indirect(part(list_out, h)), sums[m, h][:], COPY, scale=gain[:, m : m + 1]
-                )
+            fetch(x_b, table_b, list_b, step_b[:, r : r + 1], r, 0, J)
+        codes_b = keep.tile([P, J], U32, name="codes_b", align_bytes=64)
+        scales_b = keep.tile([P, J], U8, name="scales_b", align_bytes=64)
+        quantise(codes_b[:], scales_b[:], x_b, 0, J)
+        fetch(x_a, table_a, list_a, step_a[:, 0:1], 0, 0, J)
+        for r in (1, 2):
+            fetch(x_a, table_a, list_a, step_a[:, r : r + 1], r, 0, HALF)
+        turn = keep.tile([P, 1], F32, name="turn_first", tag="turn")
+        nc.vector.tensor_copy(turn[:], step_a[:, 3:4])
+        fetch(x_a, table_a, list_a, turn[:], 3, 0, HALF // 2)
+        fetch(x_a, table_a, list_a, step_a[:, 3:4], 3, HALF // 2, HALF)
+        fetch(x_a, table_a, list_a, step_a[:, 3:4], 3, HALF, J)
+
+        accs = [psum.tile([P, HALF], F32, name=f"acc{m}0", tag=f"acc{m}") for m in row_tiles]
+        for m in row_tiles:
+            multiply(accs[m], m, codes_b[:, :HALF], scales_b[:, :HALF], True)
+        codes_a = keep.tile([P, HALF], U32, name="codes_a0", tag="codes_a", align_bytes=64)
+        scales_a = keep.tile([P, HALF], U8, name="scales_a0", tag="scales_a", align_bytes=64)
+        quantise(codes_a[:, : HALF // 2], scales_a[:, : HALF // 2], x_a, 0, HALF // 2)
+        turn = keep.tile([P, 2], F32, name="turn_second", tag="turn")
+        nc.vector.tensor_copy(turn[:], step_a[:, 1:3])
+        quantise(codes_a[:, HALF // 2 :], scales_a[:, HALF // 2 :], x_a, HALF // 2, HALF)
+        for r in (1, 2):
+            fetch(x_a, table_a, list_a, turn[:, r - 1 : r], r, HALF, J)
+        for m in row_tiles:
+            multiply(accs[m], m, codes_a[:], scales_a[:], False)
+        put(0, accs)
+
+        accs = [psum.tile([P, HALF], F32, name=f"acc{m}1", tag=f"acc{m}") for m in row_tiles]
+        for m in row_tiles:
+            multiply(accs[m], m, codes_b[:, HALF:], scales_b[:, HALF:], True)
+        codes_a = keep.tile([P, HALF], U32, name="codes_a1", tag="codes_a", align_bytes=64)
+        scales_a = keep.tile([P, HALF], U8, name="scales_a1", tag="scales_a", align_bytes=64)
+        quantise(codes_a[:], scales_a[:], x_a, HALF, J)
+        for m in row_tiles:
+            multiply(accs[m], m, codes_a[:], scales_a[:], False)
+        put(1, accs)
         for m in row_tiles:
             nc.sync.dma_start(out[m * P : (m + 1) * P, :], pages[m][:])

@@ -37,31 +37,15 @@ def tile_list_twocodebooks_kernel(tc, ca, cb, sa, sb, w_words, w_scales, so, off
         step_b = keep.tile([P, PACK], F32, name="step_b")
         gain = keep.tile([P, N // P], F32, name="gain")
         table_a = [keep.tile([P, T], F32, name=f"table_a{r}") for r in range(PACK)]
-        table_b = [keep.tile([P, V], F32, name=f"table_b{r}") for r in range(PACK)]
+        pairs_b = [keep.tile([P, 2 * V], F32, name=f"pair_b{u}") for u in range(2)]
+        odd_b = [keep.tile([P, V], F32, name=f"odd_b{u}") for u in range(2)]
+        table_b = [pairs_b[0], odd_b[0], pairs_b[1], odd_b[1]]
         w_codes = keep.tile([P, 2 * N], U8, name="w_codes", align_bytes=64)
-        w_rows = keep.tile([4, 4, N // 4], I32, name="w_rows")
         w_plane = keep.tile([P, N], U8, name="w_plane", align_bytes=64)
         pages = [keep.tile([P, E], F32, name=f"page{m}") for m in row_tiles]
 
         ca_rows = ca.rearrange("(p r) t -> r p t", r=PACK)
-        cb_rows = cb.rearrange("(p r) v -> r p v", r=PACK)
-
-        nc.scalar.dma_start(step_b[:], sb.rearrange("(p r) o -> p (r o)", r=PACK))
-        nc.sync.dma_start(table_b[0][:], cb_rows[0])
-        nc.sync.dma_start(list_b[:], offs2)
-        for r in range(1, PACK):
-            nc.sync.dma_start(table_b[r][:], cb_rows[r])
-        nc.sync.dma_start(table_a[0][:], ca_rows[0])
-        nc.sync.dma_start(list_a[:], offs)
-        nc.sync.dma_start(step_a[:], sa.rearrange("(p r) o -> p (r o)", r=PACK))
-        nc.sync.dma_start(table_a[1][:], ca_rows[1])
-        nc.sync.dma_start(w_rows[:], w_scales[0].bitcast(I32).rearrange("(q r) c -> r q c", r=4))
-        for r in range(2, PACK):
-            nc.sync.dma_start(table_a[r][:], ca_rows[r])
-        nc.sync.dma_start(w_codes[:].bitcast(I32), w_words[0].bitcast(I32))
-        nc.sync.dma_start(list_out[:], offs3)
-        with nc.allow_non_contiguous_dma(reason="one float a partition and row tile"):
-            nc.sync.dma_start(gain[:], so.rearrange("(m p) o -> p (m o)", p=P))
+        cb_pairs = cb.rearrange("(p u e) v -> u p (e v)", u=2, e=2)
 
         warm_in = keep.tile([P, 1], F32, name="warm_in")
         warm_out = keep.tile([P, 1], F32, name="warm_out")
@@ -70,8 +54,27 @@ def tile_list_twocodebooks_kernel(tc, ca, cb, sa, sb, w_words, w_scales, so, off
         nc.vector.memset(w_plane[:].bitcast(I32), 0)
         for m in row_tiles:
             nc.vector.memset(pages[m][:], 0.0)
+
+        nc.scalar.dma_start(step_b[:], sb.rearrange("(p r) o -> p (r o)", r=PACK))
+        nc.sync.dma_start(pairs_b[0][:], cb_pairs[0])
+        nc.sync.dma_start(list_b[:], offs2)
+        nc.sync.dma_start(pairs_b[1][:], cb_pairs[1])
+        nc.sync.dma_start(table_a[0][:], ca_rows[0])
+        nc.sync.dma_start(list_a[:], offs)
+        nc.sync.dma_start(step_a[:], sa.rearrange("(p r) o -> p (r o)", r=PACK))
+        for r in range(1, PACK):
+            nc.sync.dma_start(table_a[r][:], ca_rows[r])
+        nc.sync.dma_start(w_codes[:].bitcast(I32), w_words[0].bitcast(I32))
         for q in range(4):
-            nc.vector.tensor_copy(w_plane[32 * q : 32 * q + 4, :].bitcast(I32), w_rows[:, q, :])
+            nc.sync.dma_start(
+                w_plane[32 * q : 32 * q + 4, :].bitcast(I32), w_scales[0, 4 * q : 4 * q + 4, :].bitcast(I32)
+            )
+        nc.sync.dma_start(list_out[:], offs3)
+        with nc.allow_non_contiguous_dma(reason="one float a partition and row tile"):
+            nc.sync.dma_start(gain[:], so.rearrange("(m p) o -> p (m o)", p=P))
+
+        for u in range(2):
+            nc.vector.tensor_copy(odd_b[u][:], pairs_b[u][:, V:])
 
         x_a = keep.tile([P, PACK * J], BF16, name="x_a", align_bytes=64)
         x_b = keep.tile([P, PACK * J], BF16, name="x_b", align_bytes=64)
@@ -114,9 +117,9 @@ def tile_list_twocodebooks_kernel(tc, ca, cb, sa, sb, w_words, w_scales, so, off
         codes_b = keep.tile([P, J], U32, name="codes_b", align_bytes=64)
         scales_b = keep.tile([P, J], U8, name="scales_b", align_bytes=64)
         quantise(codes_b[:], scales_b[:], x_b, 0, J)
-        fetch(x_a, table_a, list_a, step_a[:, 0:1], 0, 0, J)
-        for r in (1, 2):
-            fetch(x_a, table_a, list_a, step_a[:, r : r + 1], r, 0, HALF)
+        for r in (0, 1):
+            fetch(x_a, table_a, list_a, step_a[:, r : r + 1], r, 0, J)
+        fetch(x_a, table_a, list_a, step_a[:, 2:3], 2, 0, HALF)
         turn = keep.tile([P, 1], F32, name="turn_first", tag="turn")
         nc.vector.tensor_copy(turn[:], step_a[:, 3:4])
         fetch(x_a, table_a, list_a, turn[:], 3, 0, HALF // 2)
@@ -129,11 +132,10 @@ def tile_list_twocodebooks_kernel(tc, ca, cb, sa, sb, w_words, w_scales, so, off
         codes_a = keep.tile([P, HALF], U32, name="codes_a0", tag="codes_a", align_bytes=64)
         scales_a = keep.tile([P, HALF], U8, name="scales_a0", tag="scales_a", align_bytes=64)
         quantise(codes_a[:, : HALF // 2], scales_a[:, : HALF // 2], x_a, 0, HALF // 2)
-        turn = keep.tile([P, 2], F32, name="turn_second", tag="turn")
-        nc.vector.tensor_copy(turn[:], step_a[:, 1:3])
+        turn = keep.tile([P, 1], F32, name="turn_second", tag="turn")
+        nc.vector.tensor_copy(turn[:], step_a[:, 2:3])
         quantise(codes_a[:, HALF // 2 :], scales_a[:, HALF // 2 :], x_a, HALF // 2, HALF)
-        for r in (1, 2):
-            fetch(x_a, table_a, list_a, turn[:, r - 1 : r], r, HALF, J)
+        fetch(x_a, table_a, list_a, turn[:], 2, HALF, J)
         for m in row_tiles:
             multiply(accs[m], m, codes_a[:], scales_a[:], False)
         put(0, accs)

from contextlib import ExitStack

import concourse.mybir as mybir

K, T, V, J, N, E = 512, 1024, 512, 256, 256, 512
FLOPS = 2 * 2 * K * N * J

F32 = mybir.dt.float32
BF16 = mybir.dt.bfloat16
I32 = mybir.dt.int32
U32 = mybir.dt.uint32
U16 = mybir.dt.uint16
U8 = mybir.dt.uint8
FP8X4 = mybir.dt.float8_e4m3fn_x4
FP4X4 = mybir.dt.float4_e2m1fn_x4
COPY = mybir.ActivationFunctionType.Copy

P = 128
PACK = 4
HALF = 128
LIST_COLS = HALF // 16


def tile_list_twocodebooks_kernel(tc, ca, cb, sa, sb, w_words, w_scales, so, offs, offs2, offs3, out):
    nc = tc.nc
    halves = range(J // HALF)
    row_tiles = range(N // P)

    with ExitStack() as ctx:
        keep = ctx.enter_context(tc.tile_pool(name="keep", bufs=1))
        psum = ctx.enter_context(tc.psum_pool(name="psum", bufs=1))

        list_a = keep.tile([P, J // 16], U16, name="list_a")
        list_b = keep.tile([P, J // 16], U16, name="list_b")
        list_out = keep.tile([P, J // 16], U16, name="list_out")
        step_a = keep.tile([P, PACK], F32, name="step_a")
        step_b = keep.tile([P, PACK], F32, name="step_b")
        gain = keep.tile([P, N // P], F32, name="gain")
        table_a = [keep.tile([P, T], F32, name=f"table_a{r}") for r in range(PACK)]
        pairs_b = [keep.tile([P, 2 * V], F32, name=f"pair_b{u}") for u in range(2)]
        odd_b = [keep.tile([P, V], F32, name=f"odd_b{u}") for u in range(2)]
        table_b = [pairs_b[0], odd_b[0], pairs_b[1], odd_b[1]]
        w_codes = keep.tile([P, 2 * N], U8, name="w_codes", align_bytes=64)
        w_plane = keep.tile([P, N], U8, name="w_plane", align_bytes=64)
        pages = [keep.tile([P, E], F32, name=f"page{m}") for m in row_tiles]

        ca_rows = ca.rearrange("(p r) t -> r p t", r=PACK)
        cb_pairs = cb.rearrange("(p u e) v -> u p (e v)", u=2, e=2)

        warm_in = keep.tile([P, 1], F32, name="warm_in")
        warm_out = keep.tile([P, 1], F32, name="warm_out")
        nc.vector.memset(warm_in[:], 0.0)
        nc.scalar.activation(warm_out[:], warm_in[:], COPY)
        nc.vector.memset(w_plane[:].bitcast(I32), 0)
        for m in row_tiles:
            nc.vector.memset(pages[m][:], 0.0)

        nc.scalar.dma_start(step_b[:], sb.rearrange("(p r) o -> p (r o)", r=PACK))
        nc.sync.dma_start(pairs_b[0][:], cb_pairs[0])
        nc.sync.dma_start(list_b[:], offs2)
        nc.sync.dma_start(pairs_b[1][:], cb_pairs[1])
        nc.sync.dma_start(table_a[0][:], ca_rows[0])
        nc.sync.dma_start(list_a[:], offs)
        nc.sync.dma_start(step_a[:], sa.rearrange("(p r) o -> p (r o)", r=PACK))
        for r in range(1, PACK):
            nc.sync.dma_start(table_a[r][:], ca_rows[r])
        nc.sync.dma_start(w_codes[:].bitcast(I32), w_words[0].bitcast(I32))
        for q in range(4):
            nc.sync.dma_start(
                w_plane[32 * q : 32 * q + 4, :].bitcast(I32), w_scales[0, 4 * q : 4 * q + 4, :].bitcast(I32)
            )
        nc.sync.dma_start(list_out[:], offs3)
        with nc.allow_non_contiguous_dma(reason="one float a partition and row tile"):
            nc.sync.dma_start(gain[:], so.rearrange("(m p) o -> p (m o)", p=P))

        for u in range(2):
            nc.vector.tensor_copy(odd_b[u][:], pairs_b[u][:, V:])

        x_a = keep.tile([P, PACK * J], BF16, name="x_a", align_bytes=64)
        x_b = keep.tile([P, PACK * J], BF16, name="x_b", align_bytes=64)

        def fetch(x, table, lst, scale, r, lo, hi):
            nc.scalar.activation(
                x[:, PACK * lo + r : PACK * hi : PACK],
                table[r][:].indirect(lst[:, lo // 16 : hi // 16]),
                COPY,
                scale=scale,
            )

        def quantise(codes, scales, x, lo, hi):
            nc.vector.quantize_mx(out=codes.bitcast(FP8X4), scales=scales, in_=x[:, PACK * lo : PACK * hi])

        def multiply(acc, m, codes, scales, first):
            nc.tensor.matmul_mx(
                out=acc[:],
                lhsT=w_codes[:, 2 * m * P : 2 * (m + 1) * P].bitcast(FP4X4),
                lhsT_scale=w_plane[:, m * P : (m + 1) * P],
                rhs=codes.bitcast(FP8X4),
                rhs_scale=scales,
                start=first,
                stop=not first,
            )

        def put(h, accs):
            for m in row_tiles:
                sums = keep.tile([P, HALF], F32, name=f"sums{m}{h}")
                nc.vector.tensor_copy(sums[:], accs[m][:])
                nc.scalar.activation(
                    pages[m][:].indirect(list_out[:, h * LIST_COLS : (h + 1) * LIST_COLS]),
                    sums[:],
                    COPY,
                    scale=gain[:, m : m + 1],
                )

        for r in range(PACK):
            fetch(x_b, table_b, list_b, step_b[:, r : r + 1], r, 0, J)
        codes_b = keep.tile([P, J], U32, name="codes_b", align_bytes=64)
        scales_b = keep.tile([P, J], U8, name="scales_b", align_bytes=64)
        quantise(codes_b[:], scales_b[:], x_b, 0, J)
        for r in (0, 1):
            fetch(x_a, table_a, list_a, step_a[:, r : r + 1], r, 0, J)
        fetch(x_a, table_a, list_a, step_a[:, 2:3], 2, 0, HALF)
        turn = keep.tile([P, 1], F32, name="turn_first", tag="turn")
        nc.vector.tensor_copy(turn[:], step_a[:, 3:4])
        fetch(x_a, table_a, list_a, turn[:], 3, 0, HALF // 2)
        fetch(x_a, table_a, list_a, step_a[:, 3:4], 3, HALF // 2, HALF)
        fetch(x_a, table_a, list_a, step_a[:, 3:4], 3, HALF, J)

        accs = [psum.tile([P, HALF], F32, name=f"acc{m}0", tag=f"acc{m}") for m in row_tiles]
        for m in row_tiles:
            multiply(accs[m], m, codes_b[:, :HALF], scales_b[:, :HALF], True)
        codes_a = keep.tile([P, HALF], U32, name="codes_a0", tag="codes_a", align_bytes=64)
        scales_a = keep.tile([P, HALF], U8, name="scales_a0", tag="scales_a", align_bytes=64)
        quantise(codes_a[:, : HALF // 2], scales_a[:, : HALF // 2], x_a, 0, HALF // 2)
        turn = keep.tile([P, 1], F32, name="turn_second", tag="turn")
        nc.vector.tensor_copy(turn[:], step_a[:, 2:3])
        quantise(codes_a[:, HALF // 2 :], scales_a[:, HALF // 2 :], x_a, HALF // 2, HALF)
        fetch(x_a, table_a, list_a, turn[:], 2, HALF, J)
        for m in row_tiles:
            multiply(accs[m], m, codes_a[:], scales_a[:], False)
        put(0, accs)

        accs = [psum.tile([P, HALF], F32, name=f"acc{m}1", tag=f"acc{m}") for m in row_tiles]
        for m in row_tiles:
            multiply(accs[m], m, codes_b[:, HALF:], scales_b[:, HALF:], True)
        codes_a = keep.tile([P, HALF], U32, name="codes_a1", tag="codes_a", align_bytes=64)
        scales_a = keep.tile([P, HALF], U8, name="scales_a1", tag="scales_a", align_bytes=64)
        quantise(codes_a[:], scales_a[:], x_a, HALF, J)
        for m in row_tiles:
            multiply(accs[m], m, codes_a[:], scales_a[:], False)
        put(1, accs)
        for m in row_tiles:
            nc.sync.dma_start(out[m * P : (m + 1) * P, :], pages[m][:])
